import numpy as np
import ml_dtypes


def mxq(x, axis, fmt="e4m3"):
    dtype, down = {"e4m3": (ml_dtypes.float8_e4m3fn, 7), "e5m2": (ml_dtypes.float8_e5m2, 14)}[fmt]
    v = np.moveaxis(np.asarray(x, np.float32).astype(ml_dtypes.bfloat16).astype(np.float64), axis, -1)
    blocks = v.reshape(v.shape[:-1] + (-1, 32))
    amax = np.abs(blocks).max(-1, keepdims=True)
    byte = np.maximum(np.where(amax > 0, np.frexp(amax)[1] - 1 + 127, 0) - down, 1)
    scale = np.exp2(byte - 127.0)
    codes = (blocks / scale).astype(np.float32).astype(dtype).astype(np.float64)
    return np.moveaxis((codes * scale).reshape(v.shape), -1, axis)


WIDE = False


def mx_kscale(k, group=512):
    if not WIDE:
        return np.ones(k)
    levels = np.array([18, -18])
    if group != 512:
        return np.exp2(np.random.permutation(np.resize(levels, k // group))).repeat(group)
    if k % 512:
        return np.exp2(np.random.permutation(np.resize(levels, k // 32))).repeat(32)
    a = np.empty((k // 512, 16))
    for p in range(k // 512):
        a[p, :8] = np.random.permutation(np.resize(levels, 8))
        for g in range(8):
            far = levels[np.abs(levels - a[p, g]) >= 10]
            a[p, g + 8] = far[np.random.randint(len(far))]
    return np.exp2(a.ravel()).repeat(32)


def f64(x):
    return np.asarray(x).astype(np.float64)


def silu(v):
    return v / (1.0 + np.exp(-v))


G, D, M, O, N = 4, 128, 128, 128, 512


def setup_inputs():
    n = np.random.standard_normal
    s_d = mx_kscale(D, 0)
    s_o = mx_kscale(O, 0)
    return {
        "x": (n((G, D, N)) * s_d[:, None]).astype(np.float32),
        "w1": (n((G, D, M)) / np.sqrt(D) / s_d[:, None]).astype(np.float32),
        "w2": (n((G, D, M)) / np.sqrt(D) / s_d[:, None]).astype(np.float32),
        "sh": (np.random.uniform(0.1, 0.4, (G, M, 1))).astype(np.float32),
        "d0": (np.random.uniform(5.0, 9.0, (G, M, N))).astype(np.float32),
        "wo": (n((G, O, M)) / np.sqrt(O) / s_o[:, None]).astype(np.float32),
        "dy": (n((G, O, N)) * s_o[:, None]).astype(np.float32),
        "old": (0.03 * n((G, M, N))).astype(np.float32),
    }


def reference(x, w1, w2, sh, d0, wo, dy, old):
    w1q = mxq(f64(w1), 1, "e4m3")
    xq = mxq(f64(x), 1, "e4m3")
    z1 = w1q.transpose(0, 2, 1) @ xq
    w2q = mxq(f64(w2), 1, "e4m3")
    z2 = w2q.transpose(0, 2, 1) @ xq
    q1 = f64(d0) - z1
    woq = mxq(f64(wo), 1, "e4m3")
    dyq = mxq(f64(dy), 1, "e4m3")
    c0 = woq.transpose(0, 2, 1) @ dyq
    dq1 = c0 * silu(z2) / np.square(q1 * f64(sh) + 1.0) * (-1.0) * f64(sh)
    dz1 = dq1 * (-1.0)
    y = dz1 + f64(old)
    return y

@@ -1,0 +1,160 @@
+from contextlib import ExitStack
+
+import concourse.mybir as mybir
+
+G, D, M, N = 4, 128, 128, 512
+FLOPS = 3 * 2 * G * D * M * N
+
+F32 = mybir.dt.float32
+BF16 = mybir.dt.bfloat16
+U32 = mybir.dt.uint32
+U8 = mybir.dt.uint8
+FP8X4 = mybir.dt.float8_e4m3fn_x4
+ALU = mybir.AluOpType
+ACT = mybir.ActivationFunctionType
+
+P = 128
+PACK = 4
+ROWS = D // PACK
+PIECE = 128
+HALF = N // 2
+
+
+def tile_rows_bkernstudent_kernel(tc, x, w1, w2, sh, d0, wo, dy, old, out):
+    nc = tc.nc
+    with ExitStack() as ctx:
+        sb = ctx.enter_context(tc.tile_pool(name="sb", bufs=1))
+        ps = ctx.enter_context(tc.psum_pool(name="ps", bufs=1))
+        ctx.enter_context(tc.manual_schedule())
+
+        def load_packed(name, src, c0, width):
+            raw = sb.tile([P, PACK, width], F32, name=name)
+            nc.sync.dma_start(out=raw[:], in_=src.rearrange("g (p j) n -> (g p) j n", j=PACK)[:, :, c0 : c0 + width])
+            return raw
+
+        def load_group(name, src, g):
+            t = sb.tile([P, N], F32, name=name)
+            nc.sync.dma_start(out=t[:], in_=src[g])
+            return t
+
+        def interleave(name, raw, c0):
+            t = sb.tile([P, PIECE, PACK], BF16, name=name, align_bytes=64)
+            nc.vector.tensor_copy(
+                out=t[:].rearrange("p (c i) j -> p c j i", i=4),
+                in_=raw[:, :, c0 : c0 + PIECE].rearrange("p j (c i) -> p c j i", i=4),
+            )
+            return t
+
+        def quantize(name, grouped):
+            codes = sb.tile([P, PIECE], U32, name=name + "_codes", align_bytes=64)
+            scales = sb.tile([P, PIECE], U8, name=name + "_scales", align_bytes=64)
+            nc.vector.quantize_mx(out=codes[:].bitcast(FP8X4), scales=scales[:], in_=grouped[:].rearrange("p n j -> p (n j)"))
+            return codes, scales
+
+        def quantize_half(name, raw):
+            a = interleave(name + "_ga", raw, 0)
+            b = interleave(name + "_gb", raw, PIECE)
+            return [quantize(name + "_a", a), quantize(name + "_b", b)]
+
+        def product(banks, weights, pieces, first):
+            for i, piece in enumerate(pieces):
+                cols = slice((first + i) * PIECE, (first + i + 1) * PIECE)
+                for g in range(G):
+                    rows = slice(g * ROWS, (g + 1) * ROWS)
+                    nc.tensor.matmul_mx(
+                        out=banks[g][:, cols],
+                        lhsT=weights[0][rows, :].bitcast(FP8X4),
+                        lhsT_scale=weights[1][rows, :],
+                        rhs=piece[0][rows, :].bitcast(FP8X4),
+                        rhs_scale=piece[1][rows, :],
+                        start=True,
+                        stop=True,
+                    )
+
+        bank_a = [ps.tile([P, N], F32, name="bank_a%d" % g) for g in range(G)]
+        bank_b = [ps.tile([P, N], F32, name="bank_b%d" % g) for g in range(G)]
+
+        sh_rows = sb.tile([P, G * 32], F32, name="sh_rows", align_bytes=64)
+        nc.vector.memset(sh_rows[:], 0.0)
+
+        x_raw0 = load_packed("x_raw0", x, 0, HALF)
+        w2_raw = load_packed("w2_raw", w2, 0, M)
+        w1_raw = load_packed("w1_raw", w1, 0, M)
+        x_raw1 = load_packed("x_raw1", x, HALF, HALF)
+        nc.sync.dma_start(
+            out=sh_rows[0:P:32, :].rearrange("b (g i) -> b g i", i=32),
+            in_=sh.rearrange("g (b i) o -> b g (i o)", i=32),
+        )
+        wo_raw = load_packed("wo_raw", wo, 0, M)
+        d0_sb = [load_group("d0_%d" % g, d0, g) for g in range(2)]
+        dy_raw0 = load_packed("dy_raw0", dy, 0, HALF)
+        dy_raw1 = load_packed("dy_raw1", dy, HALF, HALF)
+        d0_sb = d0_sb + [load_group("d0_%d" % g, d0, g) for g in range(2, G)]
+        old_sb = [load_group("old_%d" % g, old, g) for g in range(G)]
+
+        gate = [sb.tile([P, N], F32, name="gate%d" % g) for g in range(G)]
+        dist = [sb.tile([P, N], F32, name="dist%d" % g) for g in range(G)]
+        root = [sb.tile([P, N], F32, name="root%d" % g) for g in range(G)]
+        inv = [sb.tile([P, N], F32, name="inv%d" % g) for g in range(G)]
+        inv2 = [sb.tile([P, N], F32, name="inv2_%d" % g) for g in range(G)]
+        num = [sb.tile([P, N], F32, name="num%d" % g) for g in range(G)]
+        grad = [sb.tile([P, N], F32, name="grad%d" % g) for g in range(G)]
+        res = [sb.tile([P, N], F32, name="res%d" % g) for g in range(G)]
+        sh_cols = sb.tile([P, G * 32], F32, name="sh_cols", align_bytes=64)
+
+        def silu(h):
+            cols = slice(h * HALF, (h + 1) * HALF)
+            for g in range(G):
+                nc.scalar.activation(out=gate[g][:, cols], in_=bank_a[g][:, cols], func=ACT.Silu)
+
+        def distance(g):
+            nc.vector.tensor_tensor(out=dist[g][:], in0=d0_sb[g][:], in1=bank_b[g][:], op=ALU.subtract)
+
+        def inverse_squares(groups):
+            for g in groups:
+                nc.scalar.activation(out=root[g][:], in_=dist[g][:], func=ACT.Abs_reciprocal_sqrt, scale=sh_cols[:, 32 * g : 32 * g + 1], bias=1.0)
+            for g in groups:
+                nc.scalar.activation(out=inv[g][:], in_=root[g][:], func=ACT.Square)
+            for g in groups:
+                nc.scalar.activation(out=inv2[g][:], in_=inv[g][:], func=ACT.Square)
+
+        def numerator(g):
+            nc.vector.scalar_tensor_tensor(out=num[g][:], in0=bank_a[g][:], scalar=sh_cols[:, 32 * g : 32 * g + 1], in1=gate[g][:], op0=ALU.mult, op1=ALU.mult)
+
+        def finish(parts):
+            for g, cols in parts:
+                nc.vector.tensor_tensor(out=grad[g][:, cols], in0=num[g][:, cols], in1=inv2[g][:, cols], op=ALU.mult)
+            for g, cols in parts:
+                nc.vector.tensor_tensor(out=res[g][:, cols], in0=grad[g][:, cols], in1=old_sb[g][:, cols], op=ALU.add)
+                nc.sync.dma_start(out=out[g][:, cols], in_=res[g][:, cols])
+
+        x0 = quantize_half("x0", x_raw0)
+        w2_g = interleave("w2_g", w2_raw, 0)
+        w1_g = interleave("w1_g", w1_raw, 0)
+        w2_q = quantize("w2", w2_g)
+        w1_q = quantize("w1", w1_g)
+        product(bank_a, w2_q, x0, 0)
+        product(bank_b, w1_q, x0, 0)
+        silu(0)
+        x1 = quantize_half("x1", x_raw1)
+        product(bank_a, w2_q, x1, 2)
+        product(bank_b, w1_q, x1, 2)
+        silu(1)
+        wo_g = interleave("wo_g", wo_raw, 0)
+        nc.vector.transpose(out=sh_cols[:], in_=sh_rows[:])
+        wo_q = quantize("wo", wo_g)
+        distance(0)
+        distance(1)
+        inverse_squares([0, 1])
+        dy0 = quantize_half("dy0", dy_raw0)
+        product(bank_a, wo_q, dy0, 0)
+        dy1 = quantize_half("dy1", dy_raw1)
+        product(bank_a, wo_q, dy1, 2)
+        distance(2)
+        distance(3)
+        inverse_squares([2, 3])
+        for g in range(G):
+            numerator(g)
+        whole = slice(0, N)
+        finish([(0, whole), (1, whole)])
+        finish([(2, whole), (3, slice(0, HALF)), (3, slice(HALF, N))])

@@ -37,9 +37,9 @@ def tile_rows_bkernstudent_kernel(tc, x, w1, w2, sh, d0, wo, dy, old, out):
             nc.sync.dma_start(out=t[:], in_=src[g])
             return t
 
-        def interleave(name, raw, c0):
+        def interleave(name, raw, c0, copy=nc.vector.tensor_copy):
             t = sb.tile([P, PIECE, PACK], BF16, name=name, align_bytes=64)
-            nc.vector.tensor_copy(
+            copy(
                 out=t[:].rearrange("p (c i) j -> p c j i", i=4),
                 in_=raw[:, :, c0 : c0 + PIECE].rearrange("p j (c i) -> p c j i", i=4),
             )
@@ -50,11 +50,6 @@ def tile_rows_bkernstudent_kernel(tc, x, w1, w2, sh, d0, wo, dy, old, out):
             scales = sb.tile([P, PIECE], U8, name=name + "_scales", align_bytes=64)
             nc.vector.quantize_mx(out=codes[:].bitcast(FP8X4), scales=scales[:], in_=grouped[:].rearrange("p n j -> p (n j)"))
             return codes, scales
-
-        def quantize_half(name, raw):
-            a = interleave(name + "_ga", raw, 0)
-            b = interleave(name + "_gb", raw, PIECE)
-            return [quantize(name + "_a", a), quantize(name + "_b", b)]
 
         def product(banks, weights, pieces, first):
             for i, piece in enumerate(pieces):
@@ -77,19 +72,17 @@ def tile_rows_bkernstudent_kernel(tc, x, w1, w2, sh, d0, wo, dy, old, out):
         sh_rows = sb.tile([P, G * 32], F32, name="sh_rows", align_bytes=64)
         nc.vector.memset(sh_rows[:], 0.0)
 
-        x_raw0 = load_packed("x_raw0", x, 0, HALF)
+        x_raw = load_packed("x_raw", x, 0, N)
         w2_raw = load_packed("w2_raw", w2, 0, M)
-        w1_raw = load_packed("w1_raw", w1, 0, M)
-        x_raw1 = load_packed("x_raw1", x, HALF, HALF)
+        dy_raw0 = load_packed("dy_raw0", dy, 0, HALF)
         nc.sync.dma_start(
             out=sh_rows[0:P:32, :].rearrange("b (g i) -> b g i", i=32),
             in_=sh.rearrange("g (b i) o -> b g (i o)", i=32),
         )
         wo_raw = load_packed("wo_raw", wo, 0, M)
-        d0_sb = [load_group("d0_%d" % g, d0, g) for g in range(2)]
-        dy_raw0 = load_packed("dy_raw0", dy, 0, HALF)
+        w1_raw = load_packed("w1_raw", w1, 0, M)
         dy_raw1 = load_packed("dy_raw1", dy, HALF, HALF)
-        d0_sb = d0_sb + [load_group("d0_%d" % g, d0, g) for g in range(2, G)]
+        d0_sb = [load_group("d0_%d" % g, d0, g) for g in range(G)]
         old_sb = [load_group("old_%d" % g, old, g) for g in range(G)]
 
         gate = [sb.tile([P, N], F32, name="gate%d" % g) for g in range(G)]
@@ -102,59 +95,80 @@ def tile_rows_bkernstudent_kernel(tc, x, w1, w2, sh, d0, wo, dy, old, out):
         res = [sb.tile([P, N], F32, name="res%d" % g) for g in range(G)]
         sh_cols = sb.tile([P, G * 32], F32, name="sh_cols", align_bytes=64)
 
-        def silu(h):
-            cols = slice(h * HALF, (h + 1) * HALF)
-            for g in range(G):
-                nc.scalar.activation(out=gate[g][:, cols], in_=bank_a[g][:, cols], func=ACT.Silu)
-
         def distance(g):
             nc.vector.tensor_tensor(out=dist[g][:], in0=d0_sb[g][:], in1=bank_b[g][:], op=ALU.subtract)
 
-        def inverse_squares(groups):
-            for g in groups:
-                nc.scalar.activation(out=root[g][:], in_=dist[g][:], func=ACT.Abs_reciprocal_sqrt, scale=sh_cols[:, 32 * g : 32 * g + 1], bias=1.0)
-            for g in groups:
-                nc.scalar.activation(out=inv[g][:], in_=root[g][:], func=ACT.Square)
-            for g in groups:
-                nc.scalar.activation(out=inv2[g][:], in_=inv[g][:], func=ACT.Square)
+        def inverse_squares(parts):
+            for g, cols in parts:
+                nc.scalar.activation(out=root[g][:, cols], in_=dist[g][:, cols], func=ACT.Abs_reciprocal_sqrt, scale=sh_cols[:, 32 * g : 32 * g + 1], bias=1.0)
+            for g, cols in parts:
+                nc.scalar.activation(out=inv[g][:, cols], in_=root[g][:, cols], func=ACT.Square)
+            for g, cols in parts:
+                nc.scalar.activation(out=inv2[g][:, cols], in_=inv[g][:, cols], func=ACT.Square)
 
         def numerator(g):
             nc.vector.scalar_tensor_tensor(out=num[g][:], in0=bank_a[g][:], scalar=sh_cols[:, 32 * g : 32 * g + 1], in1=gate[g][:], op0=ALU.mult, op1=ALU.mult)
 
-        def finish(parts):
-            for g, cols in parts:
-                nc.vector.tensor_tensor(out=grad[g][:, cols], in0=num[g][:, cols], in1=inv2[g][:, cols], op=ALU.mult)
-            for g, cols in parts:
-                nc.vector.tensor_tensor(out=res[g][:, cols], in0=grad[g][:, cols], in1=old_sb[g][:, cols], op=ALU.add)
-                nc.sync.dma_start(out=out[g][:, cols], in_=res[g][:, cols])
+        def gradient(g, cols):
+            nc.vector.tensor_tensor(out=grad[g][:, cols], in0=num[g][:, cols], in1=inv2[g][:, cols], op=ALU.mult)
 
-        x0 = quantize_half("x0", x_raw0)
-        w2_g = interleave("w2_g", w2_raw, 0)
-        w1_g = interleave("w1_g", w1_raw, 0)
-        w2_q = quantize("w2", w2_g)
-        w1_q = quantize("w1", w1_g)
-        product(bank_a, w2_q, x0, 0)
-        product(bank_b, w1_q, x0, 0)
-        silu(0)
-        x1 = quantize_half("x1", x_raw1)
-        product(bank_a, w2_q, x1, 2)
-        product(bank_b, w1_q, x1, 2)
-        silu(1)
-        wo_g = interleave("wo_g", wo_raw, 0)
-        nc.vector.transpose(out=sh_cols[:], in_=sh_rows[:])
-        wo_q = quantize("wo", wo_g)
-        distance(0)
-        distance(1)
-        inverse_squares([0, 1])
-        dy0 = quantize_half("dy0", dy_raw0)
-        product(bank_a, wo_q, dy0, 0)
-        dy1 = quantize_half("dy1", dy_raw1)
-        product(bank_a, wo_q, dy1, 2)
-        distance(2)
-        distance(3)
-        inverse_squares([2, 3])
-        for g in range(G):
-            numerator(g)
+        def result(g, cols):
+            nc.vector.tensor_tensor(out=res[g][:, cols], in0=grad[g][:, cols], in1=old_sb[g][:, cols], op=ALU.add)
+            nc.sync.dma_start(out=out[g][:, cols], in_=res[g][:, cols])
+
         whole = slice(0, N)
-        finish([(0, whole), (1, whole)])
-        finish([(2, whole), (3, slice(0, HALF)), (3, slice(HALF, N))])
+        halves = [slice(0, HALF), slice(HALF, N)]
+        last = [slice(0, HALF), slice(HALF, HALF + PIECE), slice(HALF + PIECE, N)]
+
+        warm = sb.tile([P, 1], F32, name="warm")
+        nc.gpsimd.memset(warm[:], 0.0)
+        nc.scalar.activation(out=warm[:], in_=warm[:], func=ACT.Silu)
+
+        xa = interleave("xa", x_raw, 0)
+        xb = interleave("xb", x_raw, PIECE)
+        xc = interleave("xc", x_raw, 2 * PIECE, nc.scalar.copy)
+        xd = interleave("xd", x_raw, 3 * PIECE, nc.scalar.copy)
+        w2_g = interleave("w2_g", w2_raw, 0)
+        xq = [quantize("xa", xa)]
+        w2_q = quantize("w2", w2_g)
+        xq = xq + [quantize("xb", xb), quantize("xc", xc), quantize("xd", xd)]
+        product(bank_a, w2_q, xq, 0)
+        ya = interleave("ya", dy_raw0, 0, nc.scalar.copy)
+        for g in range(G):
+            nc.scalar.activation(out=gate[g][:], in_=bank_a[g][:], func=ACT.Silu)
+        yb = interleave("yb", dy_raw0, PIECE)
+        wo_g = interleave("wo_g", wo_raw, 0)
+        yq = [quantize("ya", ya), quantize("yb", yb)]
+        w1_g = interleave("w1_g", w1_raw, 0)
+        wo_q = quantize("wo", wo_g)
+        nc.vector.transpose(out=sh_cols[:], in_=sh_rows[:])
+        w1_q = quantize("w1", w1_g)
+        product(bank_b, w1_q, xq, 0)
+        yc = interleave("yc", dy_raw1, 0)
+        yd = interleave("yd", dy_raw1, PIECE)
+        distance(0)
+        yq = yq + [quantize("yc", yc), quantize("yd", yd)]
+        product(bank_a, wo_q, yq, 0)
+        distance(1)
+        inverse_squares([(0, whole), (1, whole)])
+        distance(2)
+        numerator(0)
+        numerator(1)
+        distance(3)
+        inverse_squares([(2, cols) for cols in halves])
+        inverse_squares([(3, cols) for cols in last])
+        numerator(2)
+        numerator(3)
+        gradient(0, whole)
+        gradient(1, whole)
+        result(0, whole)
+        result(1, whole)
+        gradient(2, halves[0])
+        gradient(2, halves[1])
+        result(2, whole)
+        gradient(3, last[0])
+        gradient(3, last[1])
+        result(3, last[0])
+        gradient(3, last[2])
+        result(3, last[1])
+        result(3, last[2])

from contextlib import ExitStack

import concourse.mybir as mybir

G, D, M, N = 4, 128, 128, 512
FLOPS = 3 * 2 * G * D * M * N

F32 = mybir.dt.float32
BF16 = mybir.dt.bfloat16
U32 = mybir.dt.uint32
U8 = mybir.dt.uint8
FP8X4 = mybir.dt.float8_e4m3fn_x4
ALU = mybir.AluOpType
ACT = mybir.ActivationFunctionType

P = 128
PACK = 4
ROWS = D // PACK
PIECE = 128
HALF = N // 2


def tile_rows_bkernstudent_kernel(tc, x, w1, w2, sh, d0, wo, dy, old, out):
    nc = tc.nc
    with ExitStack() as ctx:
        sb = ctx.enter_context(tc.tile_pool(name="sb", bufs=1))
        ps = ctx.enter_context(tc.psum_pool(name="ps", bufs=1))
        ctx.enter_context(tc.manual_schedule())

        def load_packed(name, src, c0, width):
            raw = sb.tile([P, PACK, width], F32, name=name)
            nc.sync.dma_start(out=raw[:], in_=src.rearrange("g (p j) n -> (g p) j n", j=PACK)[:, :, c0 : c0 + width])
            return raw

        def load_group(name, src, g):
            t = sb.tile([P, N], F32, name=name)
            nc.sync.dma_start(out=t[:], in_=src[g])
            return t

        def interleave(name, raw, c0, copy=nc.vector.tensor_copy):
            t = sb.tile([P, PIECE, PACK], BF16, name=name, align_bytes=64)
            copy(
                out=t[:].rearrange("p (c i) j -> p c j i", i=4),
                in_=raw[:, :, c0 : c0 + PIECE].rearrange("p j (c i) -> p c j i", i=4),
            )
            return t

        def quantize(name, grouped):
            codes = sb.tile([P, PIECE], U32, name=name + "_codes", align_bytes=64)
            scales = sb.tile([P, PIECE], U8, name=name + "_scales", align_bytes=64)
            nc.vector.quantize_mx(out=codes[:].bitcast(FP8X4), scales=scales[:], in_=grouped[:].rearrange("p n j -> p (n j)"))
            return codes, scales

        def product(banks, weights, pieces, first):
            for i, piece in enumerate(pieces):
                cols = slice((first + i) * PIECE, (first + i + 1) * PIECE)
                for g in range(G):
                    rows = slice(g * ROWS, (g + 1) * ROWS)
                    nc.tensor.matmul_mx(
                        out=banks[g][:, cols],
                        lhsT=weights[0][rows, :].bitcast(FP8X4),
                        lhsT_scale=weights[1][rows, :],
                        rhs=piece[0][rows, :].bitcast(FP8X4),
                        rhs_scale=piece[1][rows, :],
                        start=True,
                        stop=True,
                    )

        bank_a = [ps.tile([P, N], F32, name="bank_a%d" % g) for g in range(G)]
        bank_b = [ps.tile([P, N], F32, name="bank_b%d" % g) for g in range(G)]

        sh_rows = sb.tile([P, G * 32], F32, name="sh_rows", align_bytes=64)
        nc.vector.memset(sh_rows[:], 0.0)

        x_raw = load_packed("x_raw", x, 0, N)
        w2_raw = load_packed("w2_raw", w2, 0, M)
        dy_raw0 = load_packed("dy_raw0", dy, 0, HALF)
        nc.sync.dma_start(
            out=sh_rows[0:P:32, :].rearrange("b (g i) -> b g i", i=32),
            in_=sh.rearrange("g (b i) o -> b g (i o)", i=32),
        )
        wo_raw = load_packed("wo_raw", wo, 0, M)
        w1_raw = load_packed("w1_raw", w1, 0, M)
        dy_raw1 = load_packed("dy_raw1", dy, HALF, HALF)
        d0_sb = [load_group("d0_%d" % g, d0, g) for g in range(G)]
        old_sb = [load_group("old_%d" % g, old, g) for g in range(G)]

        gate = [sb.tile([P, N], F32, name="gate%d" % g) for g in range(G)]
        dist = [sb.tile([P, N], F32, name="dist%d" % g) for g in range(G)]
        root = [sb.tile([P, N], F32, name="root%d" % g) for g in range(G)]
        inv = [sb.tile([P, N], F32, name="inv%d" % g) for g in range(G)]
        inv2 = [sb.tile([P, N], F32, name="inv2_%d" % g) for g in range(G)]
        num = [sb.tile([P, N], F32, name="num%d" % g) for g in range(G)]
        grad = [sb.tile([P, N], F32, name="grad%d" % g) for g in range(G)]
        res = [sb.tile([P, N], F32, name="res%d" % g) for g in range(G)]
        sh_cols = sb.tile([P, G * 32], F32, name="sh_cols", align_bytes=64)

        def distance(g):
            nc.vector.tensor_tensor(out=dist[g][:], in0=d0_sb[g][:], in1=bank_b[g][:], op=ALU.subtract)

        def inverse_squares(parts):
            for g, cols in parts:
                nc.scalar.activation(out=root[g][:, cols], in_=dist[g][:, cols], func=ACT.Abs_reciprocal_sqrt, scale=sh_cols[:, 32 * g : 32 * g + 1], bias=1.0)
            for g, cols in parts:
                nc.scalar.activation(out=inv[g][:, cols], in_=root[g][:, cols], func=ACT.Square)
            for g, cols in parts:
                nc.scalar.activation(out=inv2[g][:, cols], in_=inv[g][:, cols], func=ACT.Square)

        def numerator(g):
            nc.vector.scalar_tensor_tensor(out=num[g][:], in0=bank_a[g][:], scalar=sh_cols[:, 32 * g : 32 * g + 1], in1=gate[g][:], op0=ALU.mult, op1=ALU.mult)

        def gradient(g, cols):
            nc.vector.tensor_tensor(out=grad[g][:, cols], in0=num[g][:, cols], in1=inv2[g][:, cols], op=ALU.mult)

        def result(g, cols):
            nc.vector.tensor_tensor(out=res[g][:, cols], in0=grad[g][:, cols], in1=old_sb[g][:, cols], op=ALU.add)
            nc.sync.dma_start(out=out[g][:, cols], in_=res[g][:, cols])

        whole = slice(0, N)
        halves = [slice(0, HALF), slice(HALF, N)]
        last = [slice(0, HALF), slice(HALF, HALF + PIECE), slice(HALF + PIECE, N)]

        warm = sb.tile([P, 1], F32, name="warm")
        nc.gpsimd.memset(warm[:], 0.0)
        nc.scalar.activation(out=warm[:], in_=warm[:], func=ACT.Silu)

        xa = interleave("xa", x_raw, 0)
        xb = interleave("xb", x_raw, PIECE)
        xc = interleave("xc", x_raw, 2 * PIECE, nc.scalar.copy)
        xd = interleave("xd", x_raw, 3 * PIECE, nc.scalar.copy)
        w2_g = interleave("w2_g", w2_raw, 0)
        xq = [quantize("xa", xa)]
        w2_q = quantize("w2", w2_g)
        xq = xq + [quantize("xb", xb), quantize("xc", xc), quantize("xd", xd)]
        product(bank_a, w2_q, xq, 0)
        ya = interleave("ya", dy_raw0, 0, nc.scalar.copy)
        for g in range(G):
            nc.scalar.activation(out=gate[g][:], in_=bank_a[g][:], func=ACT.Silu)
        yb = interleave("yb", dy_raw0, PIECE)
        wo_g = interleave("wo_g", wo_raw, 0)
        yq = [quantize("ya", ya), quantize("yb", yb)]
        w1_g = interleave("w1_g", w1_raw, 0)
        wo_q = quantize("wo", wo_g)
        nc.vector.transpose(out=sh_cols[:], in_=sh_rows[:])
        w1_q = quantize("w1", w1_g)
        product(bank_b, w1_q, xq, 0)
        yc = interleave("yc", dy_raw1, 0)
        yd = interleave("yd", dy_raw1, PIECE)
        distance(0)
        yq = yq + [quantize("yc", yc), quantize("yd", yd)]
        product(bank_a, wo_q, yq, 0)
        distance(1)
        inverse_squares([(0, whole), (1, whole)])
        distance(2)
        numerator(0)
        numerator(1)
        distance(3)
        inverse_squares([(2, cols) for cols in halves])
        inverse_squares([(3, cols) for cols in last])
        numerator(2)
        numerator(3)
        gradient(0, whole)
        gradient(1, whole)
        result(0, whole)
        result(1, whole)
        gradient(2, halves[0])
        gradient(2, halves[1])
        result(2, whole)
        gradient(3, last[0])
        gradient(3, last[1])
        result(3, last[0])
        gradient(3, last[2])
        result(3, last[1])
        result(3, last[2])
